import numpy as np
import ml_dtypes


def mxq(x, axis, fmt="e4m3"):
    dtype, down = {"e4m3": (ml_dtypes.float8_e4m3fn, 7), "e5m2": (ml_dtypes.float8_e5m2, 14)}[fmt]
    v = np.moveaxis(np.asarray(x, np.float32).astype(ml_dtypes.bfloat16).astype(np.float64), axis, -1)
    blocks = v.reshape(v.shape[:-1] + (-1, 32))
    amax = np.abs(blocks).max(-1, keepdims=True)
    byte = np.maximum(np.where(amax > 0, np.frexp(amax)[1] - 1 + 127, 0) - down, 1)
    scale = np.exp2(byte - 127.0)
    codes = (blocks / scale).astype(np.float32).astype(dtype).astype(np.float64)
    return np.moveaxis((codes * scale).reshape(v.shape), -1, axis)


WIDE = False


def mx_kscale(k):
    if not WIDE:
        return np.ones(k)
    levels = np.array([10, -10, 5, -5, 0])
    if k % 512:
        return np.exp2(np.random.permutation(np.resize(levels, k // 32))).repeat(32)
    a = np.empty((k // 512, 16))
    for p in range(k // 512):
        a[p, :8] = np.random.permutation(np.resize(levels, 8))
        for g in range(8):
            far = levels[np.abs(levels - a[p, g]) >= 10]
            a[p, g + 8] = far[np.random.randint(len(far))]
    return np.exp2(a.ravel()).repeat(32)


def f64(x):
    return np.asarray(x).astype(np.float64)


def striped(idx):
    return np.tile(idx.reshape(-1, 16).T, (8, 1)).astype(np.uint16)


def unstriped(offs):
    return offs[:16].T.reshape(-1).astype(np.int64)


def silu(v):
    return v / (1.0 + np.exp(-np.maximum(v, -700.0)))


K, T, E, C, N = 512, 768, 8, 128, 128
TOP = 3
PAD = 64


def by_expert(wq, xq):
    return np.concatenate([wq[e].T @ xq[:, e * C:(e + 1) * C] for e in range(E)], axis=1)


def setup_inputs():
    n = np.random.standard_normal
    s = mx_kscale(K)[:, None]
    slot_token = np.empty(E * C, np.int64); pos = np.tile(E * C + np.arange(T) % PAD, (TOP, 1)); taken = np.zeros(T, np.int64)
    liked = np.random.randn(T)
    for e in np.random.permutation(E):
        free = np.flatnonzero(taken < TOP); pick = np.random.permutation(free[np.argsort(-(liked[free] + np.random.gumbel(size=free.size)))[:C]]); slot_token[e * C:(e + 1) * C] = pick
        pos[taken[pick], pick] = e * C + np.arange(C); taken[pick] += 1
    g = np.random.uniform(0.2, 0.8, (TOP, T))
    return {
        "xT": (n((K, T)) * s).astype(np.float32),
        "w": (n((E, K, N)) / np.sqrt(K) / s[None]).astype(np.float32),
        "b": (0.3 * n((N, E))).astype(np.float32),
        "gate": np.stack([np.tile(r, (N, 1)) for r in g]).astype(np.float32),
        "offs": striped(slot_token),
        "pos1": striped(pos[0]),
        "pos2": striped(pos[1]),
        "pos3": striped(pos[2]),
    }


def reference(xT, w, b, gate, offs, pos1, pos2, pos3):
    idx = unstriped(offs)
    xq = mxq(f64(xT)[:, idx], 0, "e4m3")
    y = by_expert(mxq(f64(w), 1, "e4m3"), xq)
    y = silu(y + np.repeat(f64(b), C, axis=1))
    y = np.concatenate([y, np.zeros((N, PAD))], axis=1)
    return sum(f64(gate[r]) * y[:, unstriped(p)] for r, p in enumerate((pos1, pos2, pos3)))

@@ -1,0 +1,119 @@
+from contextlib import ExitStack
+
+import concourse.mybir as mybir
+
+K, T, E, C, N = 512, 768, 8, 128, 128
+TOP, PAD = 3, 64
+S = E * C
+FLOPS = 2 * K * N * S
+
+F32 = mybir.dt.float32
+BF16 = mybir.dt.bfloat16
+U32 = mybir.dt.uint32
+U16 = mybir.dt.uint16
+U8 = mybir.dt.uint8
+FP8X4 = mybir.dt.float8_e4m3fn_x4
+MULT = mybir.AluOpType.mult
+ADD = mybir.AluOpType.add
+SILU = mybir.ActivationFunctionType.Silu
+
+P = 128
+PACK = 4
+X_CHUNK = 256
+X_ON_SCALAR = 80
+W_PAIR = 2
+SLOT_CUTS = (0, 512, 896, 1024)
+OUT_CUTS = (0, 512, 768)
+
+
+def weave(copy, dst, src):
+    copy(out=dst.rearrange("p (c i) j -> p c j i", i=4), in_=src.rearrange("p j (c i) -> p c j i", i=4))
+
+
+def tile_moe_ecr_lin_silu_kernel(tc, xT, w, b, gate, offs, pos1, pos2, pos3, out):
+    nc = tc.nc
+    with ExitStack() as ctx:
+        keep = ctx.enter_context(tc.tile_pool(name="keep", bufs=1))
+        psum = ctx.enter_context(tc.psum_pool(name="psum", bufs=1))
+
+        offs_sb = keep.tile([P, S // 16], U16, name="offs_sb")
+        pos_sb = [keep.tile([P, T // 16], U16, name="pos_sb%d" % r) for r in range(TOP)]
+
+        x_view = xT.rearrange("(p j) t -> p j t", j=PACK)
+        x_raw = []
+        for c in range(T // X_CHUNK):
+            t = keep.tile([P, PACK, X_CHUNK], F32, name="x_raw%d" % c)
+            nc.sync.dma_start(out=t[:], in_=x_view[:, :, c * X_CHUNK:(c + 1) * X_CHUNK])
+            x_raw.append(t)
+        nc.sync.dma_start(offs_sb[:], offs)
+        w_view = w.rearrange("e (p j) n -> p e j n", j=PACK)
+        w_raw = []
+        for g in range(E // W_PAIR):
+            t = keep.tile([P, W_PAIR, PACK, N], F32, name="w_raw%d" % g)
+            nc.sync.dma_start(out=t[:], in_=w_view[:, g * W_PAIR:(g + 1) * W_PAIR])
+            w_raw.append(t)
+        b_sb = keep.tile([P, E], F32, name="b_sb")
+        nc.sync.dma_start(out=b_sb[:], in_=b)
+        gate_sb = []
+        for r, pos in enumerate((pos1, pos2, pos3)):
+            nc.sync.dma_start(pos_sb[r][:], pos)
+            t = keep.tile([P, T], F32, name="gate_sb%d" % r)
+            nc.sync.dma_start(out=t[:], in_=gate[r])
+            gate_sb.append(t)
+
+        y = keep.tile([P, S + PAD], F32, name="y")
+        zeros = keep.tile([P, PAD], F32, name="zeros")
+        nc.gpsimd.memset(zeros[:], 0.0)
+        nc.scalar.activation(y[:, S:], zeros[:], SILU)
+
+        x_codes = keep.tile([P, T], U32, name="x_codes", align_bytes=64)
+        x_scales = keep.tile([P, T], U8, name="x_scales", align_bytes=64)
+        nc.gpsimd.memset(x_scales[:], 0)
+        for c in range(T // X_CHUNK):
+            xb = keep.tile([P, X_CHUNK, PACK], BF16, name="x_bf%d" % c, align_bytes=64)
+            cut = X_CHUNK - X_ON_SCALAR
+            weave(nc.vector.tensor_copy, xb[:, :cut, :], x_raw[c][:, :, :cut])
+            weave(nc.scalar.copy, xb[:, cut:, :], x_raw[c][:, :, cut:])
+            cols = slice(c * X_CHUNK, (c + 1) * X_CHUNK)
+            nc.vector.quantize_mx(out=x_codes[:, cols].bitcast(FP8X4), scales=x_scales[:, cols],
+                                  in_=xb[:].rearrange("p t j -> p (t j)"))
+
+        w_codes, w_scales = [], []
+        for g in range(E // W_PAIR):
+            wb = keep.tile([P, W_PAIR, N, PACK], BF16, name="w_bf%d" % g, align_bytes=64)
+            for i in range(W_PAIR):
+                weave(nc.scalar.copy, wb[:, i], w_raw[g][:, i])
+            wc = keep.tile([P, W_PAIR * N], U32, name="w_codes%d" % g, align_bytes=64)
+            ws = keep.tile([P, W_PAIR * N], U8, name="w_scales%d" % g, align_bytes=64)
+            w_codes.append(wc)
+            w_scales.append(ws)
+            w_bf = wb
+            nc.vector.quantize_mx(out=wc[:].bitcast(FP8X4), scales=ws[:], in_=w_bf[:].rearrange("p e n j -> p (e n j)"))
+
+        for lo, hi in zip(SLOT_CUTS, SLOT_CUTS[1:]):
+            idx = offs_sb[:, lo // 16:hi // 16]
+            s_codes = keep.tile([P, hi - lo], U32, name="s_codes%d" % lo, align_bytes=64)
+            s_scales = keep.tile([P, hi - lo], U8, name="s_scales%d" % lo, align_bytes=64)
+            nc.vector.tensor_copy(s_codes[:], x_codes[:].indirect(idx))
+            nc.vector.tensor_copy(s_scales[:], x_scales[:].indirect(idx))
+            for e in range(lo // C, hi // C):
+                acc = psum.tile([P, C], F32, name="acc%d" % e)
+                mine = slice(e * C - lo, (e + 1) * C - lo)
+                wcols = slice((e % W_PAIR) * N, (e % W_PAIR + 1) * N)
+                nc.tensor.matmul_mx(out=acc[:], lhsT=w_codes[e // W_PAIR][:, wcols].bitcast(FP8X4),
+                                    lhsT_scale=w_scales[e // W_PAIR][:, wcols],
+                                    rhs=s_codes[:, mine].bitcast(FP8X4), rhs_scale=s_scales[:, mine],
+                                    start=True, stop=True)
+                nc.scalar.activation(y[:, e * C:(e + 1) * C], acc[:], SILU, bias=b_sb[:, e:e + 1])
+
+        for lo, hi in zip(OUT_CUTS, OUT_CUTS[1:]):
+            terms = []
+            for r in range(TOP):
+                t = keep.tile([P, hi - lo], F32, name="term%d_%d" % (r, lo))
+                nc.vector.tensor_tensor(t[:], y[:].indirect(pos_sb[r][:, lo // 16:hi // 16]), gate_sb[r][:, lo:hi], MULT)
+                terms.append(t)
+            part = keep.tile([P, hi - lo], F32, name="part%d" % lo)
+            nc.vector.tensor_tensor(part[:], terms[0][:], terms[1][:], ADD)
+            res = keep.tile([P, hi - lo], F32, name="res%d" % lo)
+            nc.vector.tensor_tensor(res[:], part[:], terms[2][:], ADD)
+            nc.sync.dma_start(out=out[:, lo:hi], in_=res[:])

@@ -1,6 +1,7 @@
 from contextlib import ExitStack
 
 import concourse.mybir as mybir
+from concourse.masks import make_identity
 
 K, T, E, C, N = 512, 768, 8, 128, 128
 TOP, PAD = 3, 64
@@ -19,11 +20,13 @@ SILU = mybir.ActivationFunctionType.Silu
 
 P = 128
 PACK = 4
-X_CHUNK = 256
-X_ON_SCALAR = 80
+X_CUTS = (0, 512, 768)
+X_PIECES = ((0, 256, 0), (256, 512, 240), (512, 640, 0), (640, 768, 96))
+W_CUTS = (0, 1, 2, 4, 6, 8)
 W_PAIR = 2
 SLOT_CUTS = (0, 512, 896, 1024)
-OUT_CUTS = (0, 512, 768)
+PE_CUTS = (0, 256, 512)
+OUT_CUTS = PE_CUTS + (T,)
 
 
 def weave(copy, dst, src):
@@ -41,25 +44,26 @@ def tile_moe_ecr_lin_silu_kernel(tc, xT, w, b, gate, offs, pos1, pos2, pos3, out
 
         x_view = xT.rearrange("(p j) t -> p j t", j=PACK)
         x_raw = []
-        for c in range(T // X_CHUNK):
-            t = keep.tile([P, PACK, X_CHUNK], F32, name="x_raw%d" % c)
-            nc.sync.dma_start(out=t[:], in_=x_view[:, :, c * X_CHUNK:(c + 1) * X_CHUNK])
+        for lo, hi in zip(X_CUTS, X_CUTS[1:]):
+            t = keep.tile([P, PACK, hi - lo], F32, name="x_raw%d" % lo)
+            nc.sync.dma_start(out=t[:], in_=x_view[:, :, lo:hi])
             x_raw.append(t)
         nc.sync.dma_start(offs_sb[:], offs)
         w_view = w.rearrange("e (p j) n -> p e j n", j=PACK)
         w_raw = []
-        for g in range(E // W_PAIR):
-            t = keep.tile([P, W_PAIR, PACK, N], F32, name="w_raw%d" % g)
-            nc.sync.dma_start(out=t[:], in_=w_view[:, g * W_PAIR:(g + 1) * W_PAIR])
-            w_raw.append(t)
+        for lo, hi in zip(W_CUTS, W_CUTS[1:]):
+            t = keep.tile([P, hi - lo, PACK, N], F32, name="w_raw%d" % lo, tag="raw%d" % lo, align_bytes=64)
+            nc.sync.dma_start(out=t[:], in_=w_view[:, lo:hi])
+            w_raw.extend([t[:, i] for i in range(hi - lo)])
         b_sb = keep.tile([P, E], F32, name="b_sb")
         nc.sync.dma_start(out=b_sb[:], in_=b)
-        gate_sb = []
         for r, pos in enumerate((pos1, pos2, pos3)):
             nc.sync.dma_start(pos_sb[r][:], pos)
-            t = keep.tile([P, T], F32, name="gate_sb%d" % r)
-            nc.sync.dma_start(out=t[:], in_=gate[r])
-            gate_sb.append(t)
+        gate_sb = {}
+        gate_view = gate.rearrange("r n t -> n r t")
+        for lo, hi in zip(OUT_CUTS, OUT_CUTS[1:]):
+            gate_sb[lo] = keep.tile([P, TOP, hi - lo], F32, name="gate_sb%d" % lo)
+            nc.sync.dma_start(out=gate_sb[lo][:], in_=gate_view[:, :, lo:hi])
 
         y = keep.tile([P, S + PAD], F32, name="y")
         zeros = keep.tile([P, PAD], F32, name="zeros")
@@ -69,51 +73,88 @@ def tile_moe_ecr_lin_silu_kernel(tc, xT, w, b, gate, offs, pos1, pos2, pos3, out
         x_codes = keep.tile([P, T], U32, name="x_codes", align_bytes=64)
         x_scales = keep.tile([P, T], U8, name="x_scales", align_bytes=64)
         nc.gpsimd.memset(x_scales[:], 0)
-        for c in range(T // X_CHUNK):
-            xb = keep.tile([P, X_CHUNK, PACK], BF16, name="x_bf%d" % c, align_bytes=64)
-            cut = X_CHUNK - X_ON_SCALAR
-            weave(nc.vector.tensor_copy, xb[:, :cut, :], x_raw[c][:, :, :cut])
-            weave(nc.scalar.copy, xb[:, cut:, :], x_raw[c][:, :, cut:])
-            cols = slice(c * X_CHUNK, (c + 1) * X_CHUNK)
-            nc.vector.quantize_mx(out=x_codes[:, cols].bitcast(FP8X4), scales=x_scales[:, cols],
+        ident = keep.tile([P, P], F32, name="ident")
+        make_identity(nc, ident[:])
+        for lo, hi, on_scalar in X_PIECES:
+            c = max(i for i in range(len(x_raw)) if X_CUTS[i] <= lo)
+            src = x_raw[c][:, :, lo - X_CUTS[c]:hi - X_CUTS[c]]
+            xb = keep.tile([P, hi - lo, PACK], BF16, name="x_bf%d" % lo, align_bytes=64)
+            cut = hi - lo - on_scalar
+            weave(nc.vector.tensor_copy, xb[:, :cut, :], src[:, :, :cut])
+            if on_scalar:
+                weave(nc.scalar.copy, xb[:, cut:, :], src[:, :, cut:])
+            nc.vector.quantize_mx(out=x_codes[:, lo:hi].bitcast(FP8X4), scales=x_scales[:, lo:hi],
                                   in_=xb[:].rearrange("p t j -> p (t j)"))
 
-        w_codes, w_scales = [], []
-        for g in range(E // W_PAIR):
-            wb = keep.tile([P, W_PAIR, N, PACK], BF16, name="w_bf%d" % g, align_bytes=64)
+        w_codes, w_scales = {}, {}
+
+        def quantise_weights(g, tag):
+            wb = keep.tile([P, W_PAIR, N, PACK], BF16, name="w_bf%d" % g, tag=tag, align_bytes=64)
             for i in range(W_PAIR):
-                weave(nc.scalar.copy, wb[:, i], w_raw[g][:, i])
+                weave(nc.scalar.copy, wb[:, i], w_raw[g * W_PAIR + i])
             wc = keep.tile([P, W_PAIR * N], U32, name="w_codes%d" % g, align_bytes=64)
             ws = keep.tile([P, W_PAIR * N], U8, name="w_scales%d" % g, align_bytes=64)
-            w_codes.append(wc)
-            w_scales.append(ws)
-            w_bf = wb
-            nc.vector.quantize_mx(out=wc[:].bitcast(FP8X4), scales=ws[:], in_=w_bf[:].rearrange("p e n j -> p (e n j)"))
+            nc.vector.quantize_mx(out=wc[:].bitcast(FP8X4), scales=ws[:], in_=wb[:].rearrange("p e n j -> p (e n j)"))
+            for i in range(W_PAIR):
+                w_codes[g * W_PAIR + i] = wc[:, i * N:(i + 1) * N]
+                w_scales[g * W_PAIR + i] = ws[:, i * N:(i + 1) * N]
 
-        for lo, hi in zip(SLOT_CUTS, SLOT_CUTS[1:]):
-            idx = offs_sb[:, lo // 16:hi // 16]
-            s_codes = keep.tile([P, hi - lo], U32, name="s_codes%d" % lo, align_bytes=64)
-            s_scales = keep.tile([P, hi - lo], U8, name="s_scales%d" % lo, align_bytes=64)
-            nc.vector.tensor_copy(s_codes[:], x_codes[:].indirect(idx))
-            nc.vector.tensor_copy(s_scales[:], x_scales[:].indirect(idx))
+        def gather(lo, hi, table, dtype, tag):
+            t = keep.tile([P, hi - lo], dtype, name=tag + "_g", tag=tag, align_bytes=64)
+            nc.vector.tensor_copy(t[:], table[:].indirect(offs_sb[:, lo // 16:hi // 16]))
+            return t
+
+        def experts(lo, hi, s_codes, s_scales):
             for e in range(lo // C, hi // C):
-                acc = psum.tile([P, C], F32, name="acc%d" % e)
+                acc = psum.tile([P, C], F32, name="acc%d" % e, tag="block", bufs=6)
                 mine = slice(e * C - lo, (e + 1) * C - lo)
-                wcols = slice((e % W_PAIR) * N, (e % W_PAIR + 1) * N)
-                nc.tensor.matmul_mx(out=acc[:], lhsT=w_codes[e // W_PAIR][:, wcols].bitcast(FP8X4),
-                                    lhsT_scale=w_scales[e // W_PAIR][:, wcols],
+                nc.tensor.matmul_mx(out=acc[:], lhsT=w_codes[e].bitcast(FP8X4), lhsT_scale=w_scales[e],
                                     rhs=s_codes[:, mine].bitcast(FP8X4), rhs_scale=s_scales[:, mine],
                                     start=True, stop=True)
                 nc.scalar.activation(y[:, e * C:(e + 1) * C], acc[:], SILU, bias=b_sb[:, e:e + 1])
 
-        for lo, hi in zip(OUT_CUTS, OUT_CUTS[1:]):
-            terms = []
+        c0, c1, c2, c3 = SLOT_CUTS
+        ca = gather(c0, c1, x_codes, U32, "ca")
+        sa = gather(c0, c1, x_scales, U8, "sa")
+        quantise_weights(0, "t0")
+        quantise_weights(1, "t1")
+        quantise_weights(2, "t2")
+        quantise_weights(3, "t3")
+        experts(c0, c1, ca, sa)
+        cb = gather(c1, c2, x_codes, U32, "raw2")
+        sb = gather(c1, c2, x_scales, U8, "raw4")
+        sc = gather(c2, c3, x_scales, U8, "t2")
+        experts(c1, c2 - C, cb, sb)
+        cc = gather(c2, c3, x_codes, U32, "raw6")
+        experts(c2 - C, c2, cb[:, c2 - C - c1:], sb[:, c2 - C - c1:])
+        experts(c2, c3, cc, sc)
+
+        def term(r, lo, hi):
+            t = keep.tile([P, hi - lo], F32, name="term%d_%d" % (r, lo))
+            nc.vector.tensor_tensor(t[:], y[:].indirect(pos_sb[r][:, lo // 16:hi // 16]), gate_sb[lo][:, r, :], MULT)
+            return t
+
+        for lo, hi in zip(PE_CUTS, PE_CUTS[1:]):
+            blocks = (hi - lo) // P
+            sums = [psum.tile([P, P], F32, name="sum%d_%d" % (lo, k), tag="block", bufs=6) for k in range(blocks)]
             for r in range(TOP):
-                t = keep.tile([P, hi - lo], F32, name="term%d_%d" % (r, lo))
-                nc.vector.tensor_tensor(t[:], y[:].indirect(pos_sb[r][:, lo // 16:hi // 16]), gate_sb[r][:, lo:hi], MULT)
-                terms.append(t)
-            part = keep.tile([P, hi - lo], F32, name="part%d" % lo)
-            nc.vector.tensor_tensor(part[:], terms[0][:], terms[1][:], ADD)
+                t = term(r, lo, hi)
+                for k in range(blocks):
+                    nc.tensor.matmul(sums[k][:], t[:, k * P:(k + 1) * P], ident[:], is_transpose=True,
+                                     start=(r == 0), stop=(r == TOP - 1))
+            back = psum.tile([P, hi - lo], F32, name="back%d" % lo, tag="back", bufs=2)
+            for k in range(blocks):
+                st = keep.tile([P, P], F32, name="turned%d_%d" % (lo, k))
+                nc.scalar.copy(st[:], sums[k][:])
+                nc.tensor.transpose(back[:, k * P:(k + 1) * P], st[:], ident[:])
             res = keep.tile([P, hi - lo], F32, name="res%d" % lo)
-            nc.vector.tensor_tensor(res[:], part[:], terms[2][:], ADD)
+            nc.scalar.copy(res[:], back[:])
             nc.sync.dma_start(out=out[:, lo:hi], in_=res[:])
+
+        lo, hi = PE_CUTS[-1], T
+        terms = [term(r, lo, hi) for r in range(TOP)]
+        part = keep.tile([P, hi - lo], F32, name="part")
+        nc.vector.tensor_tensor(part[:], terms[0][:], terms[1][:], ADD)
+        res = keep.tile([P, hi - lo], F32, name="res_last")
+        nc.vector.tensor_tensor(res[:], part[:], terms[2][:], ADD)
+        nc.sync.dma_start(out=out[:, lo:hi], in_=res[:])

@@ -20,9 +20,9 @@ SILU = mybir.ActivationFunctionType.Silu
 
 P = 128
 PACK = 4
-X_CUTS = (0, 512, 768)
-X_PIECES = ((0, 256, 0), (256, 512, 240), (512, 640, 0), (640, 768, 96))
-W_CUTS = (0, 1, 2, 4, 6, 8)
+X_CUTS = (0, 256, 512, 768)
+X_PIECES = ((0, 256, 128), (256, 512, 128), (512, 640, 0), (640, 768, 96))
+W_CUTS = tuple(range(E + 1))
 W_PAIR = 2
 SLOT_CUTS = (0, 512, 896, 1024)
 PE_CUTS = (0, 256, 512)
@@ -80,7 +80,8 @@ def tile_moe_ecr_lin_silu_kernel(tc, xT, w, b, gate, offs, pos1, pos2, pos3, out
             src = x_raw[c][:, :, lo - X_CUTS[c]:hi - X_CUTS[c]]
             xb = keep.tile([P, hi - lo, PACK], BF16, name="x_bf%d" % lo, align_bytes=64)
             cut = hi - lo - on_scalar
-            weave(nc.vector.tensor_copy, xb[:, :cut, :], src[:, :, :cut])
+            if cut:
+                weave(nc.vector.tensor_copy, xb[:, :cut, :], src[:, :, :cut])
             if on_scalar:
                 weave(nc.scalar.copy, xb[:, cut:, :], src[:, :, cut:])
             nc.vector.quantize_mx(out=x_codes[:, lo:hi].bitcast(FP8X4), scales=x_scales[:, lo:hi],
@@ -88,16 +89,16 @@ def tile_moe_ecr_lin_silu_kernel(tc, xT, w, b, gate, offs, pos1, pos2, pos3, out
 
         w_codes, w_scales = {}, {}
 
-        def quantise_weights(g, tag):
-            wb = keep.tile([P, W_PAIR, N, PACK], BF16, name="w_bf%d" % g, tag=tag, align_bytes=64)
-            for i in range(W_PAIR):
-                weave(nc.scalar.copy, wb[:, i], w_raw[g * W_PAIR + i])
-            wc = keep.tile([P, W_PAIR * N], U32, name="w_codes%d" % g, align_bytes=64)
-            ws = keep.tile([P, W_PAIR * N], U8, name="w_scales%d" % g, align_bytes=64)
+        def quantise_weights(g, count, tag):
+            wb = keep.tile([P, count, N, PACK], BF16, name="w_bf%d" % g, tag=tag, align_bytes=64)
+            for i in range(count):
+                weave(nc.scalar.copy, wb[:, i], w_raw[g + i])
+            wc = keep.tile([P, count * N], U32, name="w_codes%d" % g, align_bytes=64)
+            ws = keep.tile([P, count * N], U8, name="w_scales%d" % g, align_bytes=64)
             nc.vector.quantize_mx(out=wc[:].bitcast(FP8X4), scales=ws[:], in_=wb[:].rearrange("p e n j -> p (e n j)"))
-            for i in range(W_PAIR):
-                w_codes[g * W_PAIR + i] = wc[:, i * N:(i + 1) * N]
-                w_scales[g * W_PAIR + i] = ws[:, i * N:(i + 1) * N]
+            for i in range(count):
+                w_codes[g + i] = wc[:, i * N:(i + 1) * N]
+                w_scales[g + i] = ws[:, i * N:(i + 1) * N]
 
         def gather(lo, hi, table, dtype, tag):
             t = keep.tile([P, hi - lo], dtype, name=tag + "_g", tag=tag, align_bytes=64)
@@ -116,16 +117,15 @@ def tile_moe_ecr_lin_silu_kernel(tc, xT, w, b, gate, offs, pos1, pos2, pos3, out
         c0, c1, c2, c3 = SLOT_CUTS
         ca = gather(c0, c1, x_codes, U32, "ca")
         sa = gather(c0, c1, x_scales, U8, "sa")
-        quantise_weights(0, "t0")
-        quantise_weights(1, "t1")
-        quantise_weights(2, "t2")
-        quantise_weights(3, "t3")
+        quantise_weights(0, 4, "t0")
+        quantise_weights(4, 2, "t2")
+        quantise_weights(6, 2, "t3")
         experts(c0, c1, ca, sa)
-        cb = gather(c1, c2, x_codes, U32, "raw2")
-        sb = gather(c1, c2, x_scales, U8, "raw4")
+        cb = gather(c1, c2, x_codes, U32, "raw3")
+        sb = gather(c1, c2, x_scales, U8, "raw5")
         sc = gather(c2, c3, x_scales, U8, "t2")
         experts(c1, c2 - C, cb, sb)
-        cc = gather(c2, c3, x_codes, U32, "raw6")
+        cc = gather(c2, c3, x_codes, U32, "raw7")
         experts(c2 - C, c2, cb[:, c2 - C - c1:], sb[:, c2 - C - c1:])
         experts(c2, c3, cc, sc)
 
@@ -152,9 +152,19 @@ def tile_moe_ecr_lin_silu_kernel(tc, xT, w, b, gate, offs, pos1, pos2, pos3, out
             nc.sync.dma_start(out=out[:, lo:hi], in_=res[:])
 
         lo, hi = PE_CUTS[-1], T
-        terms = [term(r, lo, hi) for r in range(TOP)]
+        half = (hi - lo) // 2
+        first, second = term(0, lo, hi), term(1, lo, hi)
         part = keep.tile([P, hi - lo], F32, name="part")
-        nc.vector.tensor_tensor(part[:], terms[0][:], terms[1][:], ADD)
-        res = keep.tile([P, hi - lo], F32, name="res_last")
-        nc.vector.tensor_tensor(res[:], part[:], terms[2][:], ADD)
-        nc.sync.dma_start(out=out[:, lo:hi], in_=res[:])
+        third = []
+        for h in range(2):
+            t = keep.tile([P, half], F32, name="third%d" % h)
+            a = lo + h * half
+            nc.vector.tensor_tensor(t[:], y[:].indirect(pos_sb[2][:, a // 16:(a + half) // 16]),
+                                    gate_sb[lo][:, 2, h * half:(h + 1) * half], MULT)
+            third.append(t)
+            if h == 0:
+                nc.vector.tensor_tensor(part[:], first[:], second[:], ADD)
+        for h in range(2):
+            res = keep.tile([P, half], F32, name="res_last%d" % h)
+            nc.vector.tensor_tensor(res[:], part[:, h * half:(h + 1) * half], third[h][:], ADD)
+            nc.sync.dma_start(out=out[:, lo + h * half:lo + (h + 1) * half], in_=res[:])

@@ -25,8 +25,7 @@ X_PIECES = ((0, 256, 128), (256, 512, 128), (512, 640, 0), (640, 768, 96))
 W_CUTS = tuple(range(E + 1))
 W_PAIR = 2
 SLOT_CUTS = (0, 512, 896, 1024)
-PE_CUTS = (0, 256, 512)
-OUT_CUTS = PE_CUTS + (T,)
+OUT_CUTS = (0, 512, 768)
 
 
 def weave(copy, dst, src):
@@ -57,13 +56,11 @@ def tile_moe_ecr_lin_silu_kernel(tc, xT, w, b, gate, offs, pos1, pos2, pos3, out
             w_raw.extend([t[:, i] for i in range(hi - lo)])
         b_sb = keep.tile([P, E], F32, name="b_sb")
         nc.sync.dma_start(out=b_sb[:], in_=b)
-        for r, pos in enumerate((pos1, pos2, pos3)):
-            nc.sync.dma_start(pos_sb[r][:], pos)
         gate_sb = {}
-        gate_view = gate.rearrange("r n t -> n r t")
-        for lo, hi in zip(OUT_CUTS, OUT_CUTS[1:]):
-            gate_sb[lo] = keep.tile([P, TOP, hi - lo], F32, name="gate_sb%d" % lo)
-            nc.sync.dma_start(out=gate_sb[lo][:], in_=gate_view[:, :, lo:hi])
+        for r, pos in ((2, pos3), (1, pos2), (0, pos1)):
+            nc.sync.dma_start(pos_sb[r][:], pos)
+            gate_sb[r] = keep.tile([P, T], F32, name="gate_sb%d" % r)
+            nc.sync.dma_start(out=gate_sb[r][:], in_=gate[r])
 
         y = keep.tile([P, S + PAD], F32, name="y")
         zeros = keep.tile([P, PAD], F32, name="zeros")
@@ -131,40 +128,31 @@ def tile_moe_ecr_lin_silu_kernel(tc, xT, w, b, gate, offs, pos1, pos2, pos3, out
 
         def term(r, lo, hi):
             t = keep.tile([P, hi - lo], F32, name="term%d_%d" % (r, lo))
-            nc.vector.tensor_tensor(t[:], y[:].indirect(pos_sb[r][:, lo // 16:hi // 16]), gate_sb[lo][:, r, :], MULT)
+            nc.vector.tensor_tensor(t[:], y[:].indirect(pos_sb[r][:, lo // 16:hi // 16]), gate_sb[r][:, lo:hi], MULT)
             return t
 
-        for lo, hi in zip(PE_CUTS, PE_CUTS[1:]):
-            blocks = (hi - lo) // P
-            sums = [psum.tile([P, P], F32, name="sum%d_%d" % (lo, k), tag="block", bufs=6) for k in range(blocks)]
-            for r in range(TOP):
-                t = term(r, lo, hi)
-                for k in range(blocks):
-                    nc.tensor.matmul(sums[k][:], t[:, k * P:(k + 1) * P], ident[:], is_transpose=True,
-                                     start=(r == 0), stop=(r == TOP - 1))
-            back = psum.tile([P, hi - lo], F32, name="back%d" % lo, tag="back", bufs=2)
-            for k in range(blocks):
-                st = keep.tile([P, P], F32, name="turned%d_%d" % (lo, k))
-                nc.scalar.copy(st[:], sums[k][:])
-                nc.tensor.transpose(back[:, k * P:(k + 1) * P], st[:], ident[:])
-            res = keep.tile([P, hi - lo], F32, name="res%d" % lo)
-            nc.scalar.copy(res[:], back[:])
-            nc.sync.dma_start(out=out[:, lo:hi], in_=res[:])
+        pieces = list(zip(OUT_CUTS, OUT_CUTS[1:]))
+        sums = [psum.tile([P, P], F32, name="sum%d" % k, tag="block", bufs=6) for k in range(T // P)]
 
-        lo, hi = PE_CUTS[-1], T
-        half = (hi - lo) // 2
-        first, second = term(0, lo, hi), term(1, lo, hi)
-        part = keep.tile([P, hi - lo], F32, name="part")
-        third = []
-        for h in range(2):
-            t = keep.tile([P, half], F32, name="third%d" % h)
-            a = lo + h * half
-            nc.vector.tensor_tensor(t[:], y[:].indirect(pos_sb[2][:, a // 16:(a + half) // 16]),
-                                    gate_sb[lo][:, 2, h * half:(h + 1) * half], MULT)
-            third.append(t)
-            if h == 0:
-                nc.vector.tensor_tensor(part[:], first[:], second[:], ADD)
-        for h in range(2):
-            res = keep.tile([P, half], F32, name="res_last%d" % h)
-            nc.vector.tensor_tensor(res[:], part[:, h * half:(h + 1) * half], third[h][:], ADD)
-            nc.sync.dma_start(out=out[:, lo + h * half:lo + (h + 1) * half], in_=res[:])
+        def add_turned(r, lo, hi):
+            t = term(r, lo, hi)
+            for k in range(lo // P, hi // P):
+                nc.tensor.matmul(sums[k][:], t[:, k * P - lo:(k + 1) * P - lo], ident[:], is_transpose=True,
+                                 start=(r == 2), stop=(r == 1))
+
+        add_turned(2, 0, T)
+        for lo, hi in pieces:
+            add_turned(1, lo, hi)
+        backs = []
+        for lo, hi in pieces:
+            back = psum.tile([P, hi - lo], F32, name="back%d" % lo, tag="back", bufs=2)
+            for k in range(lo // P, hi // P):
+                st = keep.tile([P, P], F32, name="turned%d" % k)
+                nc.scalar.copy(st[:], sums[k][:])
+                nc.tensor.transpose(back[:, k * P - lo:(k + 1) * P - lo], st[:], ident[:])
+            backs.append(back)
+        third = [term(0, lo, hi) for lo, hi in pieces]
+        for t, back, (lo, hi) in zip(third, backs, pieces):
+            res = keep.tile([P, hi - lo], F32, name="res%d" % lo)
+            nc.vector.tensor_tensor(res[:], t[:], back[:], ADD)
+            nc.sync.dma_start(out=out[:, lo:hi], in_=res[:])

from contextlib import ExitStack

import concourse.mybir as mybir
from concourse.masks import make_identity

K, T, E, C, N = 512, 768, 8, 128, 128
TOP, PAD = 3, 64
S = E * C
FLOPS = 2 * K * N * S

F32 = mybir.dt.float32
BF16 = mybir.dt.bfloat16
U32 = mybir.dt.uint32
U16 = mybir.dt.uint16
U8 = mybir.dt.uint8
FP8X4 = mybir.dt.float8_e4m3fn_x4
MULT = mybir.AluOpType.mult
ADD = mybir.AluOpType.add
SILU = mybir.ActivationFunctionType.Silu

P = 128
PACK = 4
X_CUTS = (0, 256, 512, 768)
X_PIECES = ((0, 256, 128), (256, 512, 128), (512, 640, 0), (640, 768, 96))
W_CUTS = tuple(range(E + 1))
W_PAIR = 2
SLOT_CUTS = (0, 512, 896, 1024)
OUT_CUTS = (0, 512, 768)


def weave(copy, dst, src):
    copy(out=dst.rearrange("p (c i) j -> p c j i", i=4), in_=src.rearrange("p j (c i) -> p c j i", i=4))


def tile_moe_ecr_lin_silu_kernel(tc, xT, w, b, gate, offs, pos1, pos2, pos3, out):
    nc = tc.nc
    with ExitStack() as ctx:
        keep = ctx.enter_context(tc.tile_pool(name="keep", bufs=1))
        psum = ctx.enter_context(tc.psum_pool(name="psum", bufs=1))

        offs_sb = keep.tile([P, S // 16], U16, name="offs_sb")
        pos_sb = [keep.tile([P, T // 16], U16, name="pos_sb%d" % r) for r in range(TOP)]

        x_view = xT.rearrange("(p j) t -> p j t", j=PACK)
        x_raw = []
        for lo, hi in zip(X_CUTS, X_CUTS[1:]):
            t = keep.tile([P, PACK, hi - lo], F32, name="x_raw%d" % lo)
            nc.sync.dma_start(out=t[:], in_=x_view[:, :, lo:hi])
            x_raw.append(t)
        nc.sync.dma_start(offs_sb[:], offs)
        w_view = w.rearrange("e (p j) n -> p e j n", j=PACK)
        w_raw = []
        for lo, hi in zip(W_CUTS, W_CUTS[1:]):
            t = keep.tile([P, hi - lo, PACK, N], F32, name="w_raw%d" % lo, tag="raw%d" % lo, align_bytes=64)
            nc.sync.dma_start(out=t[:], in_=w_view[:, lo:hi])
            w_raw.extend([t[:, i] for i in range(hi - lo)])
        b_sb = keep.tile([P, E], F32, name="b_sb")
        nc.sync.dma_start(out=b_sb[:], in_=b)
        gate_sb = {}
        for r, pos in ((2, pos3), (1, pos2), (0, pos1)):
            nc.sync.dma_start(pos_sb[r][:], pos)
            gate_sb[r] = keep.tile([P, T], F32, name="gate_sb%d" % r)
            nc.sync.dma_start(out=gate_sb[r][:], in_=gate[r])

        y = keep.tile([P, S + PAD], F32, name="y")
        zeros = keep.tile([P, PAD], F32, name="zeros")
        nc.gpsimd.memset(zeros[:], 0.0)
        nc.scalar.activation(y[:, S:], zeros[:], SILU)

        x_codes = keep.tile([P, T], U32, name="x_codes", align_bytes=64)
        x_scales = keep.tile([P, T], U8, name="x_scales", align_bytes=64)
        nc.gpsimd.memset(x_scales[:], 0)
        ident = keep.tile([P, P], F32, name="ident")
        make_identity(nc, ident[:])
        for lo, hi, on_scalar in X_PIECES:
            c = max(i for i in range(len(x_raw)) if X_CUTS[i] <= lo)
            src = x_raw[c][:, :, lo - X_CUTS[c]:hi - X_CUTS[c]]
            xb = keep.tile([P, hi - lo, PACK], BF16, name="x_bf%d" % lo, align_bytes=64)
            cut = hi - lo - on_scalar
            if cut:
                weave(nc.vector.tensor_copy, xb[:, :cut, :], src[:, :, :cut])
            if on_scalar:
                weave(nc.scalar.copy, xb[:, cut:, :], src[:, :, cut:])
            nc.vector.quantize_mx(out=x_codes[:, lo:hi].bitcast(FP8X4), scales=x_scales[:, lo:hi],
                                  in_=xb[:].rearrange("p t j -> p (t j)"))

        w_codes, w_scales = {}, {}

        def quantise_weights(g, count, tag):
            wb = keep.tile([P, count, N, PACK], BF16, name="w_bf%d" % g, tag=tag, align_bytes=64)
            for i in range(count):
                weave(nc.scalar.copy, wb[:, i], w_raw[g + i])
            wc = keep.tile([P, count * N], U32, name="w_codes%d" % g, align_bytes=64)
            ws = keep.tile([P, count * N], U8, name="w_scales%d" % g, align_bytes=64)
            nc.vector.quantize_mx(out=wc[:].bitcast(FP8X4), scales=ws[:], in_=wb[:].rearrange("p e n j -> p (e n j)"))
            for i in range(count):
                w_codes[g + i] = wc[:, i * N:(i + 1) * N]
                w_scales[g + i] = ws[:, i * N:(i + 1) * N]

        def gather(lo, hi, table, dtype, tag):
            t = keep.tile([P, hi - lo], dtype, name=tag + "_g", tag=tag, align_bytes=64)
            nc.vector.tensor_copy(t[:], table[:].indirect(offs_sb[:, lo // 16:hi // 16]))
            return t

        def experts(lo, hi, s_codes, s_scales):
            for e in range(lo // C, hi // C):
                acc = psum.tile([P, C], F32, name="acc%d" % e, tag="block", bufs=6)
                mine = slice(e * C - lo, (e + 1) * C - lo)
                nc.tensor.matmul_mx(out=acc[:], lhsT=w_codes[e].bitcast(FP8X4), lhsT_scale=w_scales[e],
                                    rhs=s_codes[:, mine].bitcast(FP8X4), rhs_scale=s_scales[:, mine],
                                    start=True, stop=True)
                nc.scalar.activation(y[:, e * C:(e + 1) * C], acc[:], SILU, bias=b_sb[:, e:e + 1])

        c0, c1, c2, c3 = SLOT_CUTS
        ca = gather(c0, c1, x_codes, U32, "ca")
        sa = gather(c0, c1, x_scales, U8, "sa")
        quantise_weights(0, 4, "t0")
        quantise_weights(4, 2, "t2")
        quantise_weights(6, 2, "t3")
        experts(c0, c1, ca, sa)
        cb = gather(c1, c2, x_codes, U32, "raw3")
        sb = gather(c1, c2, x_scales, U8, "raw5")
        sc = gather(c2, c3, x_scales, U8, "t2")
        experts(c1, c2 - C, cb, sb)
        cc = gather(c2, c3, x_codes, U32, "raw7")
        experts(c2 - C, c2, cb[:, c2 - C - c1:], sb[:, c2 - C - c1:])
        experts(c2, c3, cc, sc)

        def term(r, lo, hi):
            t = keep.tile([P, hi - lo], F32, name="term%d_%d" % (r, lo))
            nc.vector.tensor_tensor(t[:], y[:].indirect(pos_sb[r][:, lo // 16:hi // 16]), gate_sb[r][:, lo:hi], MULT)
            return t

        pieces = list(zip(OUT_CUTS, OUT_CUTS[1:]))
        sums = [psum.tile([P, P], F32, name="sum%d" % k, tag="block", bufs=6) for k in range(T // P)]

        def add_turned(r, lo, hi):
            t = term(r, lo, hi)
            for k in range(lo // P, hi // P):
                nc.tensor.matmul(sums[k][:], t[:, k * P - lo:(k + 1) * P - lo], ident[:], is_transpose=True,
                                 start=(r == 2), stop=(r == 1))

        add_turned(2, 0, T)
        for lo, hi in pieces:
            add_turned(1, lo, hi)
        backs = []
        for lo, hi in pieces:
            back = psum.tile([P, hi - lo], F32, name="back%d" % lo, tag="back", bufs=2)
            for k in range(lo // P, hi // P):
                st = keep.tile([P, P], F32, name="turned%d" % k)
                nc.scalar.copy(st[:], sums[k][:])
                nc.tensor.transpose(back[:, k * P - lo:(k + 1) * P - lo], st[:], ident[:])
            backs.append(back)
        third = [term(0, lo, hi) for lo, hi in pieces]
        for t, back, (lo, hi) in zip(third, backs, pieces):
            res = keep.tile([P, hi - lo], F32, name="res%d" % lo)
            nc.vector.tensor_tensor(res[:], t[:], back[:], ADD)
            nc.sync.dma_start(out=out[:, lo:hi], in_=res[:])
